import numpy as np
import ml_dtypes


def mxq(x, axis, fmt="e4m3"):
    dtype, down = {"e4m3": (ml_dtypes.float8_e4m3fn, 7), "e5m2": (ml_dtypes.float8_e5m2, 14)}[fmt]
    v = np.moveaxis(np.asarray(x, np.float32).astype(ml_dtypes.bfloat16).astype(np.float64), axis, -1)
    blocks = v.reshape(v.shape[:-1] + (-1, 32))
    amax = np.abs(blocks).max(-1, keepdims=True)
    byte = np.maximum(np.where(amax > 0, np.frexp(amax)[1] - 1 + 127, 0) - down, 1)
    scale = np.exp2(byte - 127.0)
    codes = (blocks / scale).astype(np.float32).astype(dtype).astype(np.float64)
    return np.moveaxis((codes * scale).reshape(v.shape), -1, axis)


WIDE = False


def mx_kscale(k):
    if not WIDE:
        return np.ones(k)
    levels = np.array([30, -30])
    if k % 512:
        return np.exp2(np.random.permutation(np.resize(levels, k // 32))).repeat(32)
    a = np.empty((k // 512, 16))
    for p in range(k // 512):
        a[p, :8] = np.random.permutation(np.resize(levels, 8))
        for g in range(8):
            far = levels[np.abs(levels - a[p, g]) >= 10]
            a[p, g + 8] = far[np.random.randint(len(far))]
    return np.exp2(a.ravel()).repeat(32)


def f64(x):
    return np.asarray(x).astype(np.float64)


def striped(idx):
    return np.tile(np.asarray(idx).reshape(-1, 16).T, (8, 1)).astype(np.uint16)


def unstriped(offs):
    return offs[:16].T.reshape(-1).astype(np.int64)


def bf(x):
    return np.asarray(x, np.float32).astype(ml_dtypes.bfloat16)


def planes(Y):
    r, m = Y.shape
    b = f64(bf(Y)).reshape(r // 32, 32, m)
    amax = np.abs(b).max(1)
    byte = np.clip(np.where(amax > 0, np.frexp(amax)[1] - 1 + 127 - 7, 1), 1, 254)
    codes = (b * np.exp2(127.0 - byte)[:, None, :]).reshape(r, m).astype(np.float32).astype(ml_dtypes.float8_e4m3fn).view(np.uint8)
    words = codes.reshape(r // 512, 128, 4, m).transpose(0, 1, 3, 2)
    return np.ascontiguousarray(words), np.ascontiguousarray(byte.astype(np.uint8).reshape(r // 512, 16, m))


K, J, N, T, S, V = 512, 512, 256, 1024, 1024, 1024


def setup_inputs():
    n = np.random.standard_normal
    idx = np.random.permutation(T)[:J]
    idx2 = np.random.permutation(S)[:J]
    idx3 = np.random.permutation(V)[:J]
    fj = mx_kscale(J)
    return {
        "xf": (n((K, T))).astype(np.float32),
        "ra": (np.random.uniform(0.5, 1.5, (1, J)) * fj).astype(np.float32),
        "xb": (n((K, S))).astype(np.float32),
        "gt": (n((N, V)) * np.exp(0.5 * n((1, V)))).astype(np.float32),
        "rb": (np.random.uniform(0.5, 1.5, (1, J)) / fj).astype(np.float32),
        "mom": (1.0 * n((K, N))).astype(np.float32),
        "old": (1.0 * n((K, N))).astype(np.float32),
        "offs": striped(idx),
        "offs2": striped(idx2),
        "offs3": striped(idx3),
    }


def reference(xf, ra, xb, gt, rb, mom, old, offs, offs2, offs3):
    idx = unstriped(offs)
    idx2 = unstriped(offs2)
    idx3 = unstriped(offs3)
    us = f64(xf)[:, idx] * f64(xb)[:, idx2] * f64(ra)
    uj = us.T
    gs = f64(gt)[:, idx3] * f64(rb)
    gj = gs.T
    ujq = mxq(uj, 0, "e5m2")
    gjq = mxq(gj, 0, "e5m2")
    w = ujq.T @ gjq
    u2 = 0.04 * w + 0.6 * f64(mom)
    y = f64(old) * 0.5 - u2 / (1.0 + np.abs(u2))
    words, scales = planes(y)
    return y, words, scales

@@ -1,0 +1,174 @@
+from contextlib import ExitStack
+
+import concourse.mybir as mybir
+from concourse.masks import make_identity
+
+K, J, N, T = 512, 512, 256, 1024
+FLOPS = 2 * K * J * N
+
+F32 = mybir.dt.float32
+BF16 = mybir.dt.bfloat16
+I32 = mybir.dt.int32
+U32 = mybir.dt.uint32
+U16 = mybir.dt.uint16
+U8 = mybir.dt.uint8
+E5M2X4 = mybir.dt.float8_e5m2_x4
+E4M3X4 = mybir.dt.float8_e4m3fn_x4
+ALU = mybir.AluOpType
+ACT = mybir.ActivationFunctionType
+
+P = 128
+PACK = 4
+CAST_SPLIT = 160
+
+
+def tile_list_moment_products_listed_momentum_pl_kernel(tc, xf, ra, xb, gt, rb, mom, old, offs, offs2, offs3, out_0, out_1, out_2):
+    nc = tc.nc
+    with ExitStack() as ctx:
+        keep = ctx.enter_context(tc.tile_pool(name="keep", bufs=1))
+        work = ctx.enter_context(tc.tile_pool(name="work", bufs=2))
+        psum = ctx.enter_context(tc.psum_pool(name="psum", bufs=2))
+        accp = ctx.enter_context(tc.psum_pool(name="accp", bufs=1))
+
+        list_f = keep.tile([P, J // 16], U16, name="list_f")
+        list_b = keep.tile([P, J // 16], U16, name="list_b")
+        list_g = keep.tile([P, J // 16], U16, name="list_g")
+        ra4 = keep.tile([P, PACK], F32, name="ra4")
+        rb4 = keep.tile([P, PACK], F32, name="rb4")
+        xf_t = [keep.tile([P, T], F32, name="xf%d" % t, align_bytes=64) for t in range(PACK)]
+        xb_t = [keep.tile([P, T], F32, name="xb%d" % t, align_bytes=64) for t in range(PACK)]
+        gt_t = [keep.tile([P, T], F32, name="gt%d" % h) for h in range(2)]
+        mom_first = keep.tile([P, N], F32, name="mom_first")
+        mom_rest = keep.tile([P, 3, N], F32, name="mom_rest")
+        old_sb = keep.tile([P, PACK, N], F32, name="old_sb")
+        xf_rows = xf.rearrange("(p t) c -> t p c", t=PACK)
+        xb_rows = xb.rearrange("(p t) c -> t p c", t=PACK)
+
+        nc.scalar.dma_start(out=ra4[:], in_=ra.rearrange("o (p t) -> (o p) t", t=PACK))
+        nc.scalar.dma_start(out=rb4[:], in_=rb.rearrange("o (p t) -> (o p) t", t=PACK))
+        nc.sync.dma_start(list_f[:], offs)
+        nc.sync.dma_start(out=xf_t[0][:], in_=xf_rows[0])
+        nc.sync.dma_start(list_g[:], offs3)
+        nc.sync.dma_start(out=gt_t[0][:], in_=gt[0:P, :])
+        nc.sync.dma_start(out=xf_t[1][:], in_=xf_rows[1])
+        nc.sync.dma_start(list_b[:], offs2)
+        nc.sync.dma_start(out=xb_t[0][:], in_=xb_rows[0])
+        nc.sync.dma_start(out=gt_t[1][:], in_=gt[P : 2 * P, :])
+        nc.sync.dma_start(out=xb_t[1][:], in_=xb_rows[1])
+        for t in range(2, PACK):
+            nc.sync.dma_start(out=xf_t[t][:], in_=xf_rows[t])
+            nc.sync.dma_start(out=xb_t[t][:], in_=xb_rows[t])
+        mom_rows = mom.rearrange("(p t) n -> p t n", t=PACK)
+        nc.sync.dma_start(out=mom_first[:], in_=mom_rows[:, 0, :])
+        nc.sync.dma_start(out=mom_rest[:], in_=mom_rows[:, 1:PACK, :])
+        nc.sync.dma_start(out=old_sb[:], in_=old.rearrange("(p t) n -> p t n", t=PACK))
+
+        ident = keep.tile([P, P], F32, name="ident")
+        make_identity(nc, ident[:])
+
+        ra_ps = psum.tile([P, PACK, P], F32, name="ra_ps", tag="turn")
+        for m in range(PACK):
+            nc.tensor.transpose(ra_ps[:, m, :], ra4[:, m : m + 1].to_broadcast([P, P]), ident[:])
+        ra_all = keep.tile([P, J], F32, name="ra_all")
+        nc.vector.tensor_copy(out=ra_all[:].rearrange("p (q m) -> p q m", m=PACK), in_=ra_ps[:].rearrange("p m q -> p q m"))
+
+        u_codes = keep.tile([P, K], U32, name="u_codes", align_bytes=64)
+        u_scales = keep.tile([P, K], U8, name="u_scales", align_bytes=64)
+        g_codes = keep.tile([P, N], U32, name="g_codes", align_bytes=64)
+        g_scales = keep.tile([P, N], U8, name="g_scales", align_bytes=64)
+        y = keep.tile([P, PACK, N], F32, name="y")
+        soft = keep.tile([P, PACK, N], F32, name="soft")
+        out_rows = out_0.rearrange("(p t) n -> p t n", t=PACK)
+
+        def features(t):
+            fa = keep.tile([P, J], F32, name="fa", tag="fa%d" % (t % 2))
+            nc.vector.tensor_tensor(fa[:], xf_t[t][:].indirect(list_f[:]), ra_all[:], ALU.mult)
+            fb = keep.tile([P, J], F32, name="fb", tag="slot%d" % t)
+            nc.scalar.activation(fb[:], xb_t[t][:].indirect(list_b[:]), ACT.Copy)
+            us = keep.tile([P, J], BF16, name="us", tag="slot%d" % (t + 2))
+            nc.vector.tensor_tensor(us[:], fa[:], fb[:], ALU.mult)
+            pairs = us[:].bitcast(F32)
+            u_ps = psum.tile([P, 2, P], F32, name="u_ps")
+            for e in range(2):
+                nc.tensor.transpose(u_ps[:, e, :], pairs[:, e : 2 * P : 2], ident[:])
+            return u_ps
+
+        def quantise_features(t, u_ps):
+            u_bf = keep.tile([P, J], BF16, name="u_bf", tag="xb%d" % (t + 1), align_bytes=64)
+            nc.scalar.copy(out=u_bf[:].bitcast(F32).rearrange("p (k e) -> p k e", e=2), in_=u_ps[:].rearrange("p e k -> p k e"))
+            cols = slice(t * P, (t + 1) * P)
+            nc.vector.quantize_mx(out=u_codes[:, cols].bitcast(E5M2X4), scales=u_scales[:, cols], in_=u_bf[:])
+
+        def gradients(h):
+            gs = work.tile([P, J], F32, name="gs")
+            nc.scalar.activation(gs[:], gt_t[h][:].indirect(list_g[:]), ACT.Copy)
+            g_ps = psum.tile([P, PACK, P], F32, name="g_ps", tag="turn")
+            for m in range(PACK):
+                nc.tensor.transpose(g_ps[:, m, :], gs[:, m : J : PACK], ident[:])
+            return g_ps
+
+        def quantise_gradients(h, g_ps, tag):
+            g_bf = keep.tile([P, P, PACK], BF16, name="g_bf", tag=tag, align_bytes=64)
+            nc.vector.tensor_tensor(
+                g_bf[:],
+                g_ps[:].rearrange("p m n -> p n m"),
+                rb4[:].unsqueeze(1).to_broadcast([P, P, PACK]),
+                ALU.mult,
+            )
+            cols = slice(h * P, (h + 1) * P)
+            nc.vector.quantize_mx(out=g_codes[:, cols].bitcast(E5M2X4), scales=g_scales[:, cols], in_=g_bf[:].rearrange("p n m -> p (n m)"))
+
+        def update(t, v, m):
+            w = accp.tile([P, N], F32, name="w%d" % t)
+            nc.tensor.matmul_mx(
+                out=w[:],
+                lhsT=u_codes[:, t * P : (t + 1) * P].bitcast(E5M2X4),
+                lhsT_scale=u_scales[:, t * P : (t + 1) * P],
+                rhs=g_codes[:].bitcast(E5M2X4),
+                rhs_scale=g_scales[:],
+                start=True,
+                stop=True,
+            )
+            nc.vector.scalar_tensor_tensor(v, m, 15.0, w[:], ALU.mult, ALU.add)
+            mag = work.tile([P, N], F32, name="mag")
+            nc.scalar.activation(mag[:], v, ACT.Abs)
+            root = work.tile([P, N], F32, name="root")
+            nc.scalar.activation(root[:], mag[:], ACT.Abs_reciprocal_sqrt, bias=25.0)
+            inv = work.tile([P, N], F32, name="inv")
+            nc.scalar.activation(inv[:], root[:], ACT.Square)
+            nc.vector.tensor_tensor(soft[:, t, :], v, inv[:], ALU.mult)
+
+        def finish(ts):
+            nc.vector.scalar_tensor_tensor(y[:, ts, :], old_sb[:, ts, :], 0.5, soft[:, ts, :], ALU.mult, ALU.subtract)
+            nc.sync.dma_start(out=out_rows[:, ts, :], in_=y[:, ts, :])
+
+        g_turned = [gradients(0)]
+        u_turned = [features(0)]
+        g_turned.append(gradients(1))
+        for t in range(1, PACK):
+            u_turned.append(features(t))
+            if t <= 2:
+                quantise_gradients(t - 1, g_turned[t - 1], "xf%d" % t)
+            quantise_features(t - 1, u_turned[t - 1])
+        quantise_features(PACK - 1, u_turned[PACK - 1])
+        v_first = keep.tile([P, N], F32, name="v_first", tag="fa0")
+        v_rest = keep.tile([P, 3, N], F32, name="v_rest", tag="fa1")
+        update(0, v_first[:], mom_first[:])
+        update(1, v_rest[:, 0, :], mom_rest[:, 0, :])
+        update(2, v_rest[:, 1, :], mom_rest[:, 1, :])
+        finish(slice(0, 3))
+        update(3, v_rest[:, 2, :], mom_rest[:, 2, :])
+        finish(slice(3, 4))
+
+        y_bf = keep.tile([P, N, PACK], BF16, name="y_bf", align_bytes=64)
+        y_cols = y[:].rearrange("p t n -> p n t")
+        nc.vector.tensor_copy(out=y_bf[:, :CAST_SPLIT, :], in_=y_cols[:, :CAST_SPLIT, :])
+        nc.scalar.copy(out=y_bf[:, CAST_SPLIT:, :], in_=y_cols[:, CAST_SPLIT:, :])
+        y_codes = keep.tile([P, N], U32, name="y_codes", align_bytes=64)
+        y_scales = keep.tile([P, N], U8, name="y_scales", align_bytes=64)
+        nc.vector.quantize_mx(out=y_codes[:].bitcast(E4M3X4), scales=y_scales[:], in_=y_bf[:].rearrange("p n t -> p (n t)"))
+        nc.sync.dma_start(out=out_1.rearrange("z p c r -> (z p) (c r)").bitcast(I32), in_=y_codes[:].bitcast(I32))
+        scale_rows = out_2.rearrange("z q c -> (z q) c").bitcast(I32)
+        for q in range(4):
+            eng = nc.scalar if q % 2 else nc.sync
+            eng.dma_start(out=scale_rows[4 * q : 4 * q + 4, :], in_=y_scales[32 * q : 32 * q + 4, :].bitcast(I32))

@@ -19,7 +19,7 @@ ACT = mybir.ActivationFunctionType
 
 P = 128
 PACK = 4
-CAST_SPLIT = 160
+CAST_SPLIT = 96
 
 
 def tile_list_moment_products_listed_momentum_pl_kernel(tc, xf, ra, xb, gt, rb, mom, old, offs, offs2, offs3, out_0, out_1, out_2):
@@ -38,7 +38,7 @@ def tile_list_moment_products_listed_momentum_pl_kernel(tc, xf, ra, xb, gt, rb, 
         xf_t = [keep.tile([P, T], F32, name="xf%d" % t, align_bytes=64) for t in range(PACK)]
         xb_t = [keep.tile([P, T], F32, name="xb%d" % t, align_bytes=64) for t in range(PACK)]
         gt_t = [keep.tile([P, T], F32, name="gt%d" % h) for h in range(2)]
-        mom_first = keep.tile([P, N], F32, name="mom_first")
+        mom_first = keep.tile([P, N], F32, name="mom_first", align_bytes=64)
         mom_rest = keep.tile([P, 3, N], F32, name="mom_rest")
         old_sb = keep.tile([P, PACK, N], F32, name="old_sb")
         xf_rows = xf.rearrange("(p t) c -> t p c", t=PACK)
@@ -46,22 +46,27 @@ def tile_list_moment_products_listed_momentum_pl_kernel(tc, xf, ra, xb, gt, rb, 
 
         nc.scalar.dma_start(out=ra4[:], in_=ra.rearrange("o (p t) -> (o p) t", t=PACK))
         nc.scalar.dma_start(out=rb4[:], in_=rb.rearrange("o (p t) -> (o p) t", t=PACK))
-        nc.sync.dma_start(list_f[:], offs)
-        nc.sync.dma_start(out=xf_t[0][:], in_=xf_rows[0])
         nc.sync.dma_start(list_g[:], offs3)
         nc.sync.dma_start(out=gt_t[0][:], in_=gt[0:P, :])
+        nc.sync.dma_start(list_f[:], offs)
+        nc.sync.dma_start(out=xf_t[0][:], in_=xf_rows[0])
+        nc.sync.dma_start(out=gt_t[1][:], in_=gt[P : 2 * P, :])
         nc.sync.dma_start(out=xf_t[1][:], in_=xf_rows[1])
         nc.sync.dma_start(list_b[:], offs2)
         nc.sync.dma_start(out=xb_t[0][:], in_=xb_rows[0])
-        nc.sync.dma_start(out=gt_t[1][:], in_=gt[P : 2 * P, :])
+        nc.sync.dma_start(out=xf_t[2][:], in_=xf_rows[2])
         nc.sync.dma_start(out=xb_t[1][:], in_=xb_rows[1])
-        for t in range(2, PACK):
-            nc.sync.dma_start(out=xf_t[t][:], in_=xf_rows[t])
-            nc.sync.dma_start(out=xb_t[t][:], in_=xb_rows[t])
+        nc.sync.dma_start(out=xb_t[2][:], in_=xb_rows[2])
+        nc.sync.dma_start(out=xf_t[3][:], in_=xf_rows[3])
+        nc.sync.dma_start(out=xb_t[3][:], in_=xb_rows[3])
         mom_rows = mom.rearrange("(p t) n -> p t n", t=PACK)
         nc.sync.dma_start(out=mom_first[:], in_=mom_rows[:, 0, :])
         nc.sync.dma_start(out=mom_rest[:], in_=mom_rows[:, 1:PACK, :])
         nc.sync.dma_start(out=old_sb[:], in_=old.rearrange("(p t) n -> p t n", t=PACK))
+
+        warm = keep.tile([P, 16], F32, name="warm")
+        nc.vector.memset(warm[:, 0:1], 1.0)
+        nc.scalar.activation(warm[:, 8:9], warm[:, 0:1], ACT.Abs_reciprocal_sqrt, bias=25.0)
 
         ident = keep.tile([P, P], F32, name="ident")
         make_identity(nc, ident[:])
@@ -69,35 +74,39 @@ def tile_list_moment_products_listed_momentum_pl_kernel(tc, xf, ra, xb, gt, rb, 
         ra_ps = psum.tile([P, PACK, P], F32, name="ra_ps", tag="turn")
         for m in range(PACK):
             nc.tensor.transpose(ra_ps[:, m, :], ra4[:, m : m + 1].to_broadcast([P, P]), ident[:])
-        ra_all = keep.tile([P, J], F32, name="ra_all")
+        ra_all = keep.tile([P, J], F32, name="ra_all", align_bytes=64)
         nc.vector.tensor_copy(out=ra_all[:].rearrange("p (q m) -> p q m", m=PACK), in_=ra_ps[:].rearrange("p m q -> p q m"))
 
-        u_codes = keep.tile([P, K], U32, name="u_codes", align_bytes=64)
+        u_codes = {}
         u_scales = keep.tile([P, K], U8, name="u_scales", align_bytes=64)
         g_codes = keep.tile([P, N], U32, name="g_codes", align_bytes=64)
         g_scales = keep.tile([P, N], U8, name="g_scales", align_bytes=64)
         y = keep.tile([P, PACK, N], F32, name="y")
-        soft = keep.tile([P, PACK, N], F32, name="soft")
         out_rows = out_0.rearrange("(p t) n -> p t n", t=PACK)
 
         def features(t):
             fa = keep.tile([P, J], F32, name="fa", tag="fa%d" % (t % 2))
-            nc.vector.tensor_tensor(fa[:], xf_t[t][:].indirect(list_f[:]), ra_all[:], ALU.mult)
-            fb = keep.tile([P, J], F32, name="fb", tag="slot%d" % t)
+            if t % 2:
+                nc.vector.tensor_tensor(fa[:], xf_t[t][:].indirect(list_f[:]), ra_all[:], ALU.mult)
+            else:
+                picked = keep.tile([P, J], F32, name="picked")
+                nc.scalar.activation(picked[:], xf_t[t][:].indirect(list_f[:]), ACT.Copy)
+                nc.vector.tensor_tensor(fa[:], picked[:], ra_all[:], ALU.mult)
+            fb = keep.tile([P, J], F32, name="fb", tag="fb%d" % t)
             nc.scalar.activation(fb[:], xb_t[t][:].indirect(list_b[:]), ACT.Copy)
-            us = keep.tile([P, J], BF16, name="us", tag="slot%d" % (t + 2))
+            us = keep.tile([P, J], BF16, name="us", tag=["us0", "us1", "xf3", "us0"][t], align_bytes=64)
             nc.vector.tensor_tensor(us[:], fa[:], fb[:], ALU.mult)
             pairs = us[:].bitcast(F32)
-            u_ps = psum.tile([P, 2, P], F32, name="u_ps")
+            u_ps = psum.tile([P, 2, P], F32, name="u_ps", tag="u_ps" if t < 2 else "turn")
             for e in range(2):
                 nc.tensor.transpose(u_ps[:, e, :], pairs[:, e : 2 * P : 2], ident[:])
             return u_ps
 
-        def quantise_features(t, u_ps):
-            u_bf = keep.tile([P, J], BF16, name="u_bf", tag="xb%d" % (t + 1), align_bytes=64)
-            nc.scalar.copy(out=u_bf[:].bitcast(F32).rearrange("p (k e) -> p k e", e=2), in_=u_ps[:].rearrange("p e k -> p k e"))
-            cols = slice(t * P, (t + 1) * P)
-            nc.vector.quantize_mx(out=u_codes[:, cols].bitcast(E5M2X4), scales=u_scales[:, cols], in_=u_bf[:])
+        def quantise_features(t, u_ps, u_bf, copy, codes_tag):
+            copy(out=u_bf.bitcast(F32).rearrange("p (k e) -> p k e", e=2), in_=u_ps[:].rearrange("p e k -> p k e"))
+            codes = keep.tile([P, P], U32, name="codes", tag=codes_tag, align_bytes=64)
+            nc.vector.quantize_mx(out=codes[:].bitcast(E5M2X4), scales=u_scales[:, t * P : (t + 1) * P], in_=u_bf)
+            u_codes[t] = codes[:]
 
         def gradients(h):
             gs = work.tile([P, J], F32, name="gs")
@@ -107,63 +116,91 @@ def tile_list_moment_products_listed_momentum_pl_kernel(tc, xf, ra, xb, gt, rb, 
                 nc.tensor.transpose(g_ps[:, m, :], gs[:, m : J : PACK], ident[:])
             return g_ps
 
-        def quantise_gradients(h, g_ps, tag):
-            g_bf = keep.tile([P, P, PACK], BF16, name="g_bf", tag=tag, align_bytes=64)
-            nc.vector.tensor_tensor(
-                g_bf[:],
-                g_ps[:].rearrange("p m n -> p n m"),
-                rb4[:].unsqueeze(1).to_broadcast([P, P, PACK]),
-                ALU.mult,
-            )
-            cols = slice(h * P, (h + 1) * P)
-            nc.vector.quantize_mx(out=g_codes[:, cols].bitcast(E5M2X4), scales=g_scales[:, cols], in_=g_bf[:].rearrange("p n m -> p (n m)"))
+        def quantise_gradients(turned):
+            g_bf = keep.tile([P, N, PACK], BF16, name="g_bf", tag="xf1", align_bytes=64)
+            for h, g_ps in enumerate(turned):
+                nc.vector.tensor_tensor(
+                    g_bf[:, h * P : (h + 1) * P, :],
+                    g_ps[:].rearrange("p m n -> p n m"),
+                    rb4[:].unsqueeze(1).to_broadcast([P, P, PACK]),
+                    ALU.mult,
+                )
+            nc.vector.quantize_mx(out=g_codes[:].bitcast(E5M2X4), scales=g_scales[:], in_=g_bf[:].rearrange("p n m -> p (n m)"))
 
-        def update(t, v, m):
+        def momentum(t, v, m, parts):
             w = accp.tile([P, N], F32, name="w%d" % t)
             nc.tensor.matmul_mx(
                 out=w[:],
-                lhsT=u_codes[:, t * P : (t + 1) * P].bitcast(E5M2X4),
+                lhsT=u_codes[t].bitcast(E5M2X4),
                 lhsT_scale=u_scales[:, t * P : (t + 1) * P],
                 rhs=g_codes[:].bitcast(E5M2X4),
                 rhs_scale=g_scales[:],
                 start=True,
                 stop=True,
             )
-            nc.vector.scalar_tensor_tensor(v, m, 15.0, w[:], ALU.mult, ALU.add)
-            mag = work.tile([P, N], F32, name="mag")
-            nc.scalar.activation(mag[:], v, ACT.Abs)
-            root = work.tile([P, N], F32, name="root")
-            nc.scalar.activation(root[:], mag[:], ACT.Abs_reciprocal_sqrt, bias=25.0)
-            inv = work.tile([P, N], F32, name="inv")
-            nc.scalar.activation(inv[:], root[:], ACT.Square)
-            nc.vector.tensor_tensor(soft[:, t, :], v, inv[:], ALU.mult)
+            for c in parts:
+                nc.vector.scalar_tensor_tensor(v[:, c], m[:, c], 15.0, w[:, c], ALU.mult, ALU.add)
 
-        def finish(ts):
-            nc.vector.scalar_tensor_tensor(y[:, ts, :], old_sb[:, ts, :], 0.5, soft[:, ts, :], ALU.mult, ALU.subtract)
-            nc.sync.dma_start(out=out_rows[:, ts, :], in_=y[:, ts, :])
+        def soften(pieces, square_on_vector):
+            for t, c in pieces:
+                nc.scalar.activation(mag[:, t, c], v[t][:, c], ACT.Abs)
+            for t, c in pieces:
+                nc.scalar.activation(root[:, t, c], mag[:, t, c], ACT.Abs_reciprocal_sqrt, bias=25.0)
+            for t, c in pieces:
+                if t in square_on_vector:
+                    nc.vector.tensor_tensor(half[t][:, c], v[t][:, c], root[:, t, c], ALU.mult)
+                else:
+                    nc.scalar.activation(half[t][:, c], root[:, t, c], ACT.Square)
+            for t, c in pieces:
+                other = root[:, t, c] if t in square_on_vector else v[t][:, c]
+                nc.vector.tensor_tensor(soft[t][:, c], half[t][:, c], other, ALU.mult)
+
+        def finish(ts, step, parts):
+            for c in parts:
+                nc.vector.scalar_tensor_tensor(y[:, ts, c], old_sb[:, ts, c], 0.5, step[:, :, c], ALU.mult, ALU.subtract)
 
         g_turned = [gradients(0)]
         u_turned = [features(0)]
         g_turned.append(gradients(1))
-        for t in range(1, PACK):
-            u_turned.append(features(t))
-            if t <= 2:
-                quantise_gradients(t - 1, g_turned[t - 1], "xf%d" % t)
-            quantise_features(t - 1, u_turned[t - 1])
-        quantise_features(PACK - 1, u_turned[PACK - 1])
-        v_first = keep.tile([P, N], F32, name="v_first", tag="fa0")
-        v_rest = keep.tile([P, 3, N], F32, name="v_rest", tag="fa1")
-        update(0, v_first[:], mom_first[:])
-        update(1, v_rest[:, 0, :], mom_rest[:, 0, :])
-        update(2, v_rest[:, 1, :], mom_rest[:, 1, :])
-        finish(slice(0, 3))
-        update(3, v_rest[:, 2, :], mom_rest[:, 2, :])
-        finish(slice(3, 4))
+        u_turned.append(features(1))
+        quantise_gradients(g_turned)
+        u_turned.append(features(2))
+        u_turned.append(features(3))
+        u_bf0 = keep.tile([P, J], BF16, name="u_bf0", tag="xb2", align_bytes=64)
+        u_bf12 = keep.tile([P, 2 * J], BF16, name="u_bf12", tag="xb3", align_bytes=64)
+        u_bf3 = keep.tile([P, J], BF16, name="u_bf3", align_bytes=64)
+        quantise_features(0, u_turned[0], u_bf0[:], nc.scalar.copy, "ra_all")
+        quantise_features(1, u_turned[1], u_bf12[:, :J], nc.scalar.copy, "codes1")
+        quantise_features(2, u_turned[2], u_bf12[:, J:], nc.scalar.copy, "codes2")
+        quantise_features(3, u_turned[3], u_bf3[:], nc.vector.tensor_copy, "codes3")
+        whole = slice(0, N)
+        halves = [slice(0, CAST_SPLIT), slice(CAST_SPLIT, N)]
+        v_first = keep.tile([P, N], F32, name="v_first", tag="fa1")
+        after_q3 = keep.tile([P, PACK, N], F32, name="after_q3", tag="u_bf3", align_bytes=64)
+        after_v3 = keep.tile([P, PACK, N], F32, name="after_v3", tag="mom_rest")
+        v = [v_first[:]] + [after_q3[:, t, :] for t in range(1, PACK)]
+        soft = [after_q3[:, 0, :]] + [after_v3[:, t, :] for t in range(1, PACK)]
+        mag = keep.tile([P, PACK, N], F32, name="mag", tag="xf3", align_bytes=64)
+        root = keep.tile([P, PACK, N], F32, name="root")
+        squares = keep.tile([P, PACK, N], F32, name="squares")
+        half = [squares[:, 0, :], squares[:, 1, :], after_v3[:, 0, :], squares[:, 3, :]]
+        momentum(0, v[0], mom_first[:], [whole])
+        momentum(1, v[1], mom_rest[:, 0, :], [whole])
+        momentum(2, v[2], mom_rest[:, 1, :], [whole])
+        momentum(3, v[3], mom_rest[:, 2, :], halves)
+        soften([(0, whole)], ())
+        soften([(1, whole), (2, whole)], (2,))
+        finish(slice(0, 1), after_q3[:, 0:1, :], [whole])
+        finish(slice(1, 3), after_v3[:, 1:3, :], [whole])
+        nc.sync.dma_start(out=out_rows[:, 0:3, :], in_=y[:, 0:3, :])
+        soften([(3, c) for c in halves], ())
+        finish(slice(3, 4), after_v3[:, 3:4, :], halves)
+        nc.sync.dma_start(out=out_rows[:, 3, :], in_=y[:, 3, :])
 
         y_bf = keep.tile([P, N, PACK], BF16, name="y_bf", align_bytes=64)
         y_cols = y[:].rearrange("p t n -> p n t")
-        nc.vector.tensor_copy(out=y_bf[:, :CAST_SPLIT, :], in_=y_cols[:, :CAST_SPLIT, :])
-        nc.scalar.copy(out=y_bf[:, CAST_SPLIT:, :], in_=y_cols[:, CAST_SPLIT:, :])
+        nc.scalar.copy(out=y_bf[:, :CAST_SPLIT, :], in_=y_cols[:, :CAST_SPLIT, :])
+        nc.vector.tensor_copy(out=y_bf[:, CAST_SPLIT:, :], in_=y_cols[:, CAST_SPLIT:, :])
         y_codes = keep.tile([P, N], U32, name="y_codes", align_bytes=64)
         y_scales = keep.tile([P, N], U8, name="y_scales", align_bytes=64)
         nc.vector.quantize_mx(out=y_codes[:].bitcast(E4M3X4), scales=y_scales[:], in_=y_bf[:].rearrange("p n t -> p (n t)"))

@@ -52,9 +52,9 @@ def tile_list_moment_products_listed_momentum_pl_kernel(tc, xf, ra, xb, gt, rb, 
         nc.sync.dma_start(out=xf_t[0][:], in_=xf_rows[0])
         nc.sync.dma_start(out=gt_t[1][:], in_=gt[P : 2 * P, :])
         nc.sync.dma_start(out=xf_t[1][:], in_=xf_rows[1])
+        nc.sync.dma_start(out=xf_t[2][:], in_=xf_rows[2])
         nc.sync.dma_start(list_b[:], offs2)
         nc.sync.dma_start(out=xb_t[0][:], in_=xb_rows[0])
-        nc.sync.dma_start(out=xf_t[2][:], in_=xf_rows[2])
         nc.sync.dma_start(out=xb_t[1][:], in_=xb_rows[1])
         nc.sync.dma_start(out=xb_t[2][:], in_=xb_rows[2])
         nc.sync.dma_start(out=xf_t[3][:], in_=xf_rows[3])
@@ -85,16 +85,11 @@ def tile_list_moment_products_listed_momentum_pl_kernel(tc, xf, ra, xb, gt, rb, 
         out_rows = out_0.rearrange("(p t) n -> p t n", t=PACK)
 
         def features(t):
-            fa = keep.tile([P, J], F32, name="fa", tag="fa%d" % (t % 2))
-            if t % 2:
-                nc.vector.tensor_tensor(fa[:], xf_t[t][:].indirect(list_f[:]), ra_all[:], ALU.mult)
-            else:
-                picked = keep.tile([P, J], F32, name="picked")
-                nc.scalar.activation(picked[:], xf_t[t][:].indirect(list_f[:]), ACT.Copy)
-                nc.vector.tensor_tensor(fa[:], picked[:], ra_all[:], ALU.mult)
+            fa = keep.tile([P, J], F32, name="fa", tag="fa%d" % (t % 3))
+            nc.vector.tensor_tensor(fa[:], xf_t[t][:].indirect(list_f[:]), ra_all[:], ALU.mult)
             fb = keep.tile([P, J], F32, name="fb", tag="fb%d" % t)
             nc.scalar.activation(fb[:], xb_t[t][:].indirect(list_b[:]), ACT.Copy)
-            us = keep.tile([P, J], BF16, name="us", tag=["us0", "us1", "xf3", "us0"][t], align_bytes=64)
+            us = keep.tile([P, J], BF16, name="us", tag=["us0", "us1", "xf3", "us3"][t], align_bytes=64)
             nc.vector.tensor_tensor(us[:], fa[:], fb[:], ALU.mult)
             pairs = us[:].bitcast(F32)
             u_ps = psum.tile([P, 2, P], F32, name="u_ps", tag="u_ps" if t < 2 else "turn")
@@ -117,7 +112,7 @@ def tile_list_moment_products_listed_momentum_pl_kernel(tc, xf, ra, xb, gt, rb, 
             return g_ps
 
         def quantise_gradients(turned):
-            g_bf = keep.tile([P, N, PACK], BF16, name="g_bf", tag="xf1", align_bytes=64)
+            g_bf = keep.tile([P, N, PACK], BF16, name="g_bf", tag="xf2", align_bytes=64)
             for h, g_ps in enumerate(turned):
                 nc.vector.tensor_tensor(
                     g_bf[:, h * P : (h + 1) * P, :],
@@ -143,53 +138,52 @@ def tile_list_moment_products_listed_momentum_pl_kernel(tc, xf, ra, xb, gt, rb, 
 
         def soften(pieces, square_on_vector):
             for t, c in pieces:
-                nc.scalar.activation(mag[:, t, c], v[t][:, c], ACT.Abs)
+                nc.scalar.activation(mag[t][:, c], v[t][:, c], ACT.Abs)
             for t, c in pieces:
-                nc.scalar.activation(root[:, t, c], mag[:, t, c], ACT.Abs_reciprocal_sqrt, bias=25.0)
+                nc.scalar.activation(root[t][:, c], mag[t][:, c], ACT.Abs_reciprocal_sqrt, bias=25.0)
             for t, c in pieces:
                 if t in square_on_vector:
-                    nc.vector.tensor_tensor(half[t][:, c], v[t][:, c], root[:, t, c], ALU.mult)
+                    nc.vector.tensor_tensor(half[t][:, c], v[t][:, c], root[t][:, c], ALU.mult)
                 else:
-                    nc.scalar.activation(half[t][:, c], root[:, t, c], ACT.Square)
+                    nc.scalar.activation(half[t][:, c], root[t][:, c], ACT.Square)
             for t, c in pieces:
-                other = root[:, t, c] if t in square_on_vector else v[t][:, c]
+                other = root[t][:, c] if t in square_on_vector else v[t][:, c]
                 nc.vector.tensor_tensor(soft[t][:, c], half[t][:, c], other, ALU.mult)
 
         def finish(ts, step, parts):
             for c in parts:
                 nc.vector.scalar_tensor_tensor(y[:, ts, c], old_sb[:, ts, c], 0.5, step[:, :, c], ALU.mult, ALU.subtract)
 
-        g_turned = [gradients(0)]
-        u_turned = [features(0)]
-        g_turned.append(gradients(1))
-        u_turned.append(features(1))
+        g_turned = [gradients(h) for h in range(2)]
+        u_turned = [features(t) for t in range(PACK)]
         quantise_gradients(g_turned)
-        u_turned.append(features(2))
-        u_turned.append(features(3))
         u_bf0 = keep.tile([P, J], BF16, name="u_bf0", tag="xb2", align_bytes=64)
         u_bf12 = keep.tile([P, 2 * J], BF16, name="u_bf12", tag="xb3", align_bytes=64)
         u_bf3 = keep.tile([P, J], BF16, name="u_bf3", align_bytes=64)
         quantise_features(0, u_turned[0], u_bf0[:], nc.scalar.copy, "ra_all")
         quantise_features(1, u_turned[1], u_bf12[:, :J], nc.scalar.copy, "codes1")
         quantise_features(2, u_turned[2], u_bf12[:, J:], nc.scalar.copy, "codes2")
-        quantise_features(3, u_turned[3], u_bf3[:], nc.vector.tensor_copy, "codes3")
+        quantise_features(3, u_turned[3], u_bf3[:], nc.scalar.copy, "codes3")
         whole = slice(0, N)
         halves = [slice(0, CAST_SPLIT), slice(CAST_SPLIT, N)]
-        v_first = keep.tile([P, N], F32, name="v_first", tag="fa1")
+        v_first = keep.tile([P, N], F32, name="v_first", tag="fa0")
         after_q3 = keep.tile([P, PACK, N], F32, name="after_q3", tag="u_bf3", align_bytes=64)
-        after_v3 = keep.tile([P, PACK, N], F32, name="after_v3", tag="mom_rest")
-        v = [v_first[:]] + [after_q3[:, t, :] for t in range(1, PACK)]
+        after_v3 = keep.tile([P, PACK + 1, N], F32, name="after_v3", tag="mom_rest")
+        v_second = keep.tile([P, N], F32, name="v_second")
+        v = [v_first[:], v_second[:], after_q3[:, 2, :], after_q3[:, 3, :]]
         soft = [after_q3[:, 0, :]] + [after_v3[:, t, :] for t in range(1, PACK)]
-        mag = keep.tile([P, PACK, N], F32, name="mag", tag="xf3", align_bytes=64)
-        root = keep.tile([P, PACK, N], F32, name="root")
-        squares = keep.tile([P, PACK, N], F32, name="squares")
-        half = [squares[:, 0, :], squares[:, 1, :], after_v3[:, 0, :], squares[:, 3, :]]
+        mag_first = keep.tile([P, N], F32, name="mag_first", tag="xf3", align_bytes=64)
+        after_t3 = keep.tile([P, 2, PACK, N], F32, name="after_t3", tag="us3", align_bytes=64)
+        mag = [mag_first[:]] + [after_t3[:, 0, t, :] for t in range(1, PACK)]
+        root = [after_t3[:, 1, t, :] for t in range(PACK)]
+        squares = keep.tile([P, 2, N], F32, name="squares")
+        half = [squares[:, 0, :], after_v3[:, 0, :], after_v3[:, PACK, :], squares[:, 1, :]]
         momentum(0, v[0], mom_first[:], [whole])
         momentum(1, v[1], mom_rest[:, 0, :], [whole])
         momentum(2, v[2], mom_rest[:, 1, :], [whole])
         momentum(3, v[3], mom_rest[:, 2, :], halves)
         soften([(0, whole)], ())
-        soften([(1, whole), (2, whole)], (2,))
+        soften([(1, whole), (2, whole)], (1, 2))
         finish(slice(0, 1), after_q3[:, 0:1, :], [whole])
         finish(slice(1, 3), after_v3[:, 1:3, :], [whole])
         nc.sync.dma_start(out=out_rows[:, 0:3, :], in_=y[:, 0:3, :])

@@ -37,7 +37,7 @@ def tile_list_moment_products_listed_momentum_pl_kernel(tc, xf, ra, xb, gt, rb, 
         rb4 = keep.tile([P, PACK], F32, name="rb4")
         xf_t = [keep.tile([P, T], F32, name="xf%d" % t, align_bytes=64) for t in range(PACK)]
         xb_t = [keep.tile([P, T], F32, name="xb%d" % t, align_bytes=64) for t in range(PACK)]
-        gt_t = [keep.tile([P, T], F32, name="gt%d" % h) for h in range(2)]
+        gt_sb = keep.tile([P, 2, T], F32, name="gt_sb")
         mom_first = keep.tile([P, N], F32, name="mom_first", align_bytes=64)
         mom_rest = keep.tile([P, 3, N], F32, name="mom_rest")
         old_sb = keep.tile([P, PACK, N], F32, name="old_sb")
@@ -47,10 +47,9 @@ def tile_list_moment_products_listed_momentum_pl_kernel(tc, xf, ra, xb, gt, rb, 
         nc.scalar.dma_start(out=ra4[:], in_=ra.rearrange("o (p t) -> (o p) t", t=PACK))
         nc.scalar.dma_start(out=rb4[:], in_=rb.rearrange("o (p t) -> (o p) t", t=PACK))
         nc.sync.dma_start(list_g[:], offs3)
-        nc.sync.dma_start(out=gt_t[0][:], in_=gt[0:P, :])
+        nc.sync.dma_start(out=gt_sb[:], in_=gt.rearrange("(h p) c -> p h c", p=P))
         nc.sync.dma_start(list_f[:], offs)
         nc.sync.dma_start(out=xf_t[0][:], in_=xf_rows[0])
-        nc.sync.dma_start(out=gt_t[1][:], in_=gt[P : 2 * P, :])
         nc.sync.dma_start(out=xf_t[1][:], in_=xf_rows[1])
         nc.sync.dma_start(out=xf_t[2][:], in_=xf_rows[2])
         nc.sync.dma_start(list_b[:], offs2)
@@ -87,7 +86,7 @@ def tile_list_moment_products_listed_momentum_pl_kernel(tc, xf, ra, xb, gt, rb, 
         def features(t):
             fa = keep.tile([P, J], F32, name="fa", tag="fa%d" % (t % 3))
             nc.vector.tensor_tensor(fa[:], xf_t[t][:].indirect(list_f[:]), ra_all[:], ALU.mult)
-            fb = keep.tile([P, J], F32, name="fb", tag="fb%d" % t)
+            fb = keep.tile([P, J], F32, name="fb", tag="fb%d" % t, align_bytes=64)
             nc.scalar.activation(fb[:], xb_t[t][:].indirect(list_b[:]), ACT.Copy)
             us = keep.tile([P, J], BF16, name="us", tag=["us0", "us1", "xf3", "us3"][t], align_bytes=64)
             nc.vector.tensor_tensor(us[:], fa[:], fb[:], ALU.mult)
@@ -105,22 +104,22 @@ def tile_list_moment_products_listed_momentum_pl_kernel(tc, xf, ra, xb, gt, rb, 
 
         def gradients(h):
             gs = work.tile([P, J], F32, name="gs")
-            nc.scalar.activation(gs[:], gt_t[h][:].indirect(list_g[:]), ACT.Copy)
+            nc.scalar.activation(gs[:], gt_sb[:, h, :].indirect(list_g[:]), ACT.Copy)
             g_ps = psum.tile([P, PACK, P], F32, name="g_ps", tag="turn")
             for m in range(PACK):
                 nc.tensor.transpose(g_ps[:, m, :], gs[:, m : J : PACK], ident[:])
             return g_ps
 
-        def quantise_gradients(turned):
-            g_bf = keep.tile([P, N, PACK], BF16, name="g_bf", tag="xf2", align_bytes=64)
-            for h, g_ps in enumerate(turned):
-                nc.vector.tensor_tensor(
-                    g_bf[:, h * P : (h + 1) * P, :],
-                    g_ps[:].rearrange("p m n -> p n m"),
-                    rb4[:].unsqueeze(1).to_broadcast([P, P, PACK]),
-                    ALU.mult,
-                )
-            nc.vector.quantize_mx(out=g_codes[:].bitcast(E5M2X4), scales=g_scales[:], in_=g_bf[:].rearrange("p n m -> p (n m)"))
+        def quantise_gradients(h, g_ps, tag):
+            g_bf = keep.tile([P, P, PACK], BF16, name="g_bf", tag=tag, align_bytes=64)
+            nc.vector.tensor_tensor(
+                g_bf[:],
+                g_ps[:].rearrange("p m n -> p n m"),
+                rb4[:].unsqueeze(1).to_broadcast([P, P, PACK]),
+                ALU.mult,
+            )
+            cols = slice(h * P, (h + 1) * P)
+            nc.vector.quantize_mx(out=g_codes[:, cols].bitcast(E5M2X4), scales=g_scales[:, cols], in_=g_bf[:].rearrange("p n m -> p (n m)"))
 
         def momentum(t, v, m, parts):
             w = accp.tile([P, N], F32, name="w%d" % t)
@@ -156,7 +155,8 @@ def tile_list_moment_products_listed_momentum_pl_kernel(tc, xf, ra, xb, gt, rb, 
 
         g_turned = [gradients(h) for h in range(2)]
         u_turned = [features(t) for t in range(PACK)]
-        quantise_gradients(g_turned)
+        quantise_gradients(0, g_turned[0], "xf2")
+        quantise_gradients(1, g_turned[1], "fb0")
         u_bf0 = keep.tile([P, J], BF16, name="u_bf0", tag="xb2", align_bytes=64)
         u_bf12 = keep.tile([P, 2 * J], BF16, name="u_bf12", tag="xb3", align_bytes=64)
         u_bf3 = keep.tile([P, J], BF16, name="u_bf3", align_bytes=64)
@@ -168,7 +168,7 @@ def tile_list_moment_products_listed_momentum_pl_kernel(tc, xf, ra, xb, gt, rb, 
         halves = [slice(0, CAST_SPLIT), slice(CAST_SPLIT, N)]
         v_first = keep.tile([P, N], F32, name="v_first", tag="fa0")
         after_q3 = keep.tile([P, PACK, N], F32, name="after_q3", tag="u_bf3", align_bytes=64)
-        after_v3 = keep.tile([P, PACK + 1, N], F32, name="after_v3", tag="mom_rest")
+        after_v3 = keep.tile([P, PACK, N], F32, name="after_v3", tag="mom_rest")
         v_second = keep.tile([P, N], F32, name="v_second")
         v = [v_first[:], v_second[:], after_q3[:, 2, :], after_q3[:, 3, :]]
         soft = [after_q3[:, 0, :]] + [after_v3[:, t, :] for t in range(1, PACK)]
@@ -176,16 +176,18 @@ def tile_list_moment_products_listed_momentum_pl_kernel(tc, xf, ra, xb, gt, rb, 
         after_t3 = keep.tile([P, 2, PACK, N], F32, name="after_t3", tag="us3", align_bytes=64)
         mag = [mag_first[:]] + [after_t3[:, 0, t, :] for t in range(1, PACK)]
         root = [after_t3[:, 1, t, :] for t in range(PACK)]
-        squares = keep.tile([P, 2, N], F32, name="squares")
-        half = [squares[:, 0, :], after_v3[:, 0, :], after_v3[:, PACK, :], squares[:, 1, :]]
+        squares = keep.tile([P, 3, N], F32, name="squares")
+        half = [squares[:, 0, :], squares[:, 1, :], after_v3[:, 0, :], squares[:, 2, :]]
         momentum(0, v[0], mom_first[:], [whole])
         momentum(1, v[1], mom_rest[:, 0, :], [whole])
         momentum(2, v[2], mom_rest[:, 1, :], [whole])
         momentum(3, v[3], mom_rest[:, 2, :], halves)
         soften([(0, whole)], ())
-        soften([(1, whole), (2, whole)], (1, 2))
+        soften([(1, whole)], ())
+        soften([(2, whole)], (2,))
         finish(slice(0, 1), after_q3[:, 0:1, :], [whole])
-        finish(slice(1, 3), after_v3[:, 1:3, :], [whole])
+        finish(slice(1, 2), after_v3[:, 1:2, :], [whole])
+        finish(slice(2, 3), after_v3[:, 2:3, :], [whole])
         nc.sync.dma_start(out=out_rows[:, 0:3, :], in_=y[:, 0:3, :])
         soften([(3, c) for c in halves], ())
         finish(slice(3, 4), after_v3[:, 3:4, :], halves)

from contextlib import ExitStack

import concourse.mybir as mybir
from concourse.masks import make_identity

K, J, N, T = 512, 512, 256, 1024
FLOPS = 2 * K * J * N

F32 = mybir.dt.float32
BF16 = mybir.dt.bfloat16
I32 = mybir.dt.int32
U32 = mybir.dt.uint32
U16 = mybir.dt.uint16
U8 = mybir.dt.uint8
E5M2X4 = mybir.dt.float8_e5m2_x4
E4M3X4 = mybir.dt.float8_e4m3fn_x4
ALU = mybir.AluOpType
ACT = mybir.ActivationFunctionType

P = 128
PACK = 4
CAST_SPLIT = 96


def tile_list_moment_products_listed_momentum_pl_kernel(tc, xf, ra, xb, gt, rb, mom, old, offs, offs2, offs3, out_0, out_1, out_2):
    nc = tc.nc
    with ExitStack() as ctx:
        keep = ctx.enter_context(tc.tile_pool(name="keep", bufs=1))
        work = ctx.enter_context(tc.tile_pool(name="work", bufs=2))
        psum = ctx.enter_context(tc.psum_pool(name="psum", bufs=2))
        accp = ctx.enter_context(tc.psum_pool(name="accp", bufs=1))

        list_f = keep.tile([P, J // 16], U16, name="list_f")
        list_b = keep.tile([P, J // 16], U16, name="list_b")
        list_g = keep.tile([P, J // 16], U16, name="list_g")
        ra4 = keep.tile([P, PACK], F32, name="ra4")
        rb4 = keep.tile([P, PACK], F32, name="rb4")
        xf_t = [keep.tile([P, T], F32, name="xf%d" % t, align_bytes=64) for t in range(PACK)]
        xb_t = [keep.tile([P, T], F32, name="xb%d" % t, align_bytes=64) for t in range(PACK)]
        gt_sb = keep.tile([P, 2, T], F32, name="gt_sb")
        mom_first = keep.tile([P, N], F32, name="mom_first", align_bytes=64)
        mom_rest = keep.tile([P, 3, N], F32, name="mom_rest")
        old_sb = keep.tile([P, PACK, N], F32, name="old_sb")
        xf_rows = xf.rearrange("(p t) c -> t p c", t=PACK)
        xb_rows = xb.rearrange("(p t) c -> t p c", t=PACK)

        nc.scalar.dma_start(out=ra4[:], in_=ra.rearrange("o (p t) -> (o p) t", t=PACK))
        nc.scalar.dma_start(out=rb4[:], in_=rb.rearrange("o (p t) -> (o p) t", t=PACK))
        nc.sync.dma_start(list_g[:], offs3)
        nc.sync.dma_start(out=gt_sb[:], in_=gt.rearrange("(h p) c -> p h c", p=P))
        nc.sync.dma_start(list_f[:], offs)
        nc.sync.dma_start(out=xf_t[0][:], in_=xf_rows[0])
        nc.sync.dma_start(out=xf_t[1][:], in_=xf_rows[1])
        nc.sync.dma_start(out=xf_t[2][:], in_=xf_rows[2])
        nc.sync.dma_start(list_b[:], offs2)
        nc.sync.dma_start(out=xb_t[0][:], in_=xb_rows[0])
        nc.sync.dma_start(out=xb_t[1][:], in_=xb_rows[1])
        nc.sync.dma_start(out=xb_t[2][:], in_=xb_rows[2])
        nc.sync.dma_start(out=xf_t[3][:], in_=xf_rows[3])
        nc.sync.dma_start(out=xb_t[3][:], in_=xb_rows[3])
        mom_rows = mom.rearrange("(p t) n -> p t n", t=PACK)
        nc.sync.dma_start(out=mom_first[:], in_=mom_rows[:, 0, :])
        nc.sync.dma_start(out=mom_rest[:], in_=mom_rows[:, 1:PACK, :])
        nc.sync.dma_start(out=old_sb[:], in_=old.rearrange("(p t) n -> p t n", t=PACK))

        warm = keep.tile([P, 16], F32, name="warm")
        nc.vector.memset(warm[:, 0:1], 1.0)
        nc.scalar.activation(warm[:, 8:9], warm[:, 0:1], ACT.Abs_reciprocal_sqrt, bias=25.0)

        ident = keep.tile([P, P], F32, name="ident")
        make_identity(nc, ident[:])

        ra_ps = psum.tile([P, PACK, P], F32, name="ra_ps", tag="turn")
        for m in range(PACK):
            nc.tensor.transpose(ra_ps[:, m, :], ra4[:, m : m + 1].to_broadcast([P, P]), ident[:])
        ra_all = keep.tile([P, J], F32, name="ra_all", align_bytes=64)
        nc.vector.tensor_copy(out=ra_all[:].rearrange("p (q m) -> p q m", m=PACK), in_=ra_ps[:].rearrange("p m q -> p q m"))

        u_codes = {}
        u_scales = keep.tile([P, K], U8, name="u_scales", align_bytes=64)
        g_codes = keep.tile([P, N], U32, name="g_codes", align_bytes=64)
        g_scales = keep.tile([P, N], U8, name="g_scales", align_bytes=64)
        y = keep.tile([P, PACK, N], F32, name="y")
        out_rows = out_0.rearrange("(p t) n -> p t n", t=PACK)

        def features(t):
            fa = keep.tile([P, J], F32, name="fa", tag="fa%d" % (t % 3))
            nc.vector.tensor_tensor(fa[:], xf_t[t][:].indirect(list_f[:]), ra_all[:], ALU.mult)
            fb = keep.tile([P, J], F32, name="fb", tag="fb%d" % t, align_bytes=64)
            nc.scalar.activation(fb[:], xb_t[t][:].indirect(list_b[:]), ACT.Copy)
            us = keep.tile([P, J], BF16, name="us", tag=["us0", "us1", "xf3", "us3"][t], align_bytes=64)
            nc.vector.tensor_tensor(us[:], fa[:], fb[:], ALU.mult)
            pairs = us[:].bitcast(F32)
            u_ps = psum.tile([P, 2, P], F32, name="u_ps", tag="u_ps" if t < 2 else "turn")
            for e in range(2):
                nc.tensor.transpose(u_ps[:, e, :], pairs[:, e : 2 * P : 2], ident[:])
            return u_ps

        def quantise_features(t, u_ps, u_bf, copy, codes_tag):
            copy(out=u_bf.bitcast(F32).rearrange("p (k e) -> p k e", e=2), in_=u_ps[:].rearrange("p e k -> p k e"))
            codes = keep.tile([P, P], U32, name="codes", tag=codes_tag, align_bytes=64)
            nc.vector.quantize_mx(out=codes[:].bitcast(E5M2X4), scales=u_scales[:, t * P : (t + 1) * P], in_=u_bf)
            u_codes[t] = codes[:]

        def gradients(h):
            gs = work.tile([P, J], F32, name="gs")
            nc.scalar.activation(gs[:], gt_sb[:, h, :].indirect(list_g[:]), ACT.Copy)
            g_ps = psum.tile([P, PACK, P], F32, name="g_ps", tag="turn")
            for m in range(PACK):
                nc.tensor.transpose(g_ps[:, m, :], gs[:, m : J : PACK], ident[:])
            return g_ps

        def quantise_gradients(h, g_ps, tag):
            g_bf = keep.tile([P, P, PACK], BF16, name="g_bf", tag=tag, align_bytes=64)
            nc.vector.tensor_tensor(
                g_bf[:],
                g_ps[:].rearrange("p m n -> p n m"),
                rb4[:].unsqueeze(1).to_broadcast([P, P, PACK]),
                ALU.mult,
            )
            cols = slice(h * P, (h + 1) * P)
            nc.vector.quantize_mx(out=g_codes[:, cols].bitcast(E5M2X4), scales=g_scales[:, cols], in_=g_bf[:].rearrange("p n m -> p (n m)"))

        def momentum(t, v, m, parts):
            w = accp.tile([P, N], F32, name="w%d" % t)
            nc.tensor.matmul_mx(
                out=w[:],
                lhsT=u_codes[t].bitcast(E5M2X4),
                lhsT_scale=u_scales[:, t * P : (t + 1) * P],
                rhs=g_codes[:].bitcast(E5M2X4),
                rhs_scale=g_scales[:],
                start=True,
                stop=True,
            )
            for c in parts:
                nc.vector.scalar_tensor_tensor(v[:, c], m[:, c], 15.0, w[:, c], ALU.mult, ALU.add)

        def soften(pieces, square_on_vector):
            for t, c in pieces:
                nc.scalar.activation(mag[t][:, c], v[t][:, c], ACT.Abs)
            for t, c in pieces:
                nc.scalar.activation(root[t][:, c], mag[t][:, c], ACT.Abs_reciprocal_sqrt, bias=25.0)
            for t, c in pieces:
                if t in square_on_vector:
                    nc.vector.tensor_tensor(half[t][:, c], v[t][:, c], root[t][:, c], ALU.mult)
                else:
                    nc.scalar.activation(half[t][:, c], root[t][:, c], ACT.Square)
            for t, c in pieces:
                other = root[t][:, c] if t in square_on_vector else v[t][:, c]
                nc.vector.tensor_tensor(soft[t][:, c], half[t][:, c], other, ALU.mult)

        def finish(ts, step, parts):
            for c in parts:
                nc.vector.scalar_tensor_tensor(y[:, ts, c], old_sb[:, ts, c], 0.5, step[:, :, c], ALU.mult, ALU.subtract)

        g_turned = [gradients(h) for h in range(2)]
        u_turned = [features(t) for t in range(PACK)]
        quantise_gradients(0, g_turned[0], "xf2")
        quantise_gradients(1, g_turned[1], "fb0")
        u_bf0 = keep.tile([P, J], BF16, name="u_bf0", tag="xb2", align_bytes=64)
        u_bf12 = keep.tile([P, 2 * J], BF16, name="u_bf12", tag="xb3", align_bytes=64)
        u_bf3 = keep.tile([P, J], BF16, name="u_bf3", align_bytes=64)
        quantise_features(0, u_turned[0], u_bf0[:], nc.scalar.copy, "ra_all")
        quantise_features(1, u_turned[1], u_bf12[:, :J], nc.scalar.copy, "codes1")
        quantise_features(2, u_turned[2], u_bf12[:, J:], nc.scalar.copy, "codes2")
        quantise_features(3, u_turned[3], u_bf3[:], nc.scalar.copy, "codes3")
        whole = slice(0, N)
        halves = [slice(0, CAST_SPLIT), slice(CAST_SPLIT, N)]
        v_first = keep.tile([P, N], F32, name="v_first", tag="fa0")
        after_q3 = keep.tile([P, PACK, N], F32, name="after_q3", tag="u_bf3", align_bytes=64)
        after_v3 = keep.tile([P, PACK, N], F32, name="after_v3", tag="mom_rest")
        v_second = keep.tile([P, N], F32, name="v_second")
        v = [v_first[:], v_second[:], after_q3[:, 2, :], after_q3[:, 3, :]]
        soft = [after_q3[:, 0, :]] + [after_v3[:, t, :] for t in range(1, PACK)]
        mag_first = keep.tile([P, N], F32, name="mag_first", tag="xf3", align_bytes=64)
        after_t3 = keep.tile([P, 2, PACK, N], F32, name="after_t3", tag="us3", align_bytes=64)
        mag = [mag_first[:]] + [after_t3[:, 0, t, :] for t in range(1, PACK)]
        root = [after_t3[:, 1, t, :] for t in range(PACK)]
        squares = keep.tile([P, 3, N], F32, name="squares")
        half = [squares[:, 0, :], squares[:, 1, :], after_v3[:, 0, :], squares[:, 2, :]]
        momentum(0, v[0], mom_first[:], [whole])
        momentum(1, v[1], mom_rest[:, 0, :], [whole])
        momentum(2, v[2], mom_rest[:, 1, :], [whole])
        momentum(3, v[3], mom_rest[:, 2, :], halves)
        soften([(0, whole)], ())
        soften([(1, whole)], ())
        soften([(2, whole)], (2,))
        finish(slice(0, 1), after_q3[:, 0:1, :], [whole])
        finish(slice(1, 2), after_v3[:, 1:2, :], [whole])
        finish(slice(2, 3), after_v3[:, 2:3, :], [whole])
        nc.sync.dma_start(out=out_rows[:, 0:3, :], in_=y[:, 0:3, :])
        soften([(3, c) for c in halves], ())
        finish(slice(3, 4), after_v3[:, 3:4, :], halves)
        nc.sync.dma_start(out=out_rows[:, 3, :], in_=y[:, 3, :])

        y_bf = keep.tile([P, N, PACK], BF16, name="y_bf", align_bytes=64)
        y_cols = y[:].rearrange("p t n -> p n t")
        nc.scalar.copy(out=y_bf[:, :CAST_SPLIT, :], in_=y_cols[:, :CAST_SPLIT, :])
        nc.vector.tensor_copy(out=y_bf[:, CAST_SPLIT:, :], in_=y_cols[:, CAST_SPLIT:, :])
        y_codes = keep.tile([P, N], U32, name="y_codes", align_bytes=64)
        y_scales = keep.tile([P, N], U8, name="y_scales", align_bytes=64)
        nc.vector.quantize_mx(out=y_codes[:].bitcast(E4M3X4), scales=y_scales[:], in_=y_bf[:].rearrange("p n t -> p (n t)"))
        nc.sync.dma_start(out=out_1.rearrange("z p c r -> (z p) (c r)").bitcast(I32), in_=y_codes[:].bitcast(I32))
        scale_rows = out_2.rearrange("z q c -> (z q) c").bitcast(I32)
        for q in range(4):
            eng = nc.scalar if q % 2 else nc.sync
            eng.dma_start(out=scale_rows[4 * q : 4 * q + 4, :], in_=y_scales[32 * q : 32 * q + 4, :].bitcast(I32))
